import numpy as np
import ml_dtypes


def mxq(x, axis, fmt="e4m3"):
    dtype, down = {"e4m3": (ml_dtypes.float8_e4m3fn, 7), "e5m2": (ml_dtypes.float8_e5m2, 14)}[fmt]
    v = np.moveaxis(np.asarray(x, np.float32).astype(ml_dtypes.bfloat16).astype(np.float64), axis, -1)
    blocks = v.reshape(v.shape[:-1] + (-1, 32))
    amax = np.abs(blocks).max(-1, keepdims=True)
    byte = np.maximum(np.where(amax > 0, np.frexp(amax)[1] - 1 + 127, 0) - down, 1)
    scale = np.exp2(byte - 127.0)
    codes = (blocks / scale).astype(np.float32).astype(dtype).astype(np.float64)
    return np.moveaxis((codes * scale).reshape(v.shape), -1, axis)


WIDE = False


def mx_kscale(k):
    if not WIDE:
        return np.ones(k)
    levels = np.array([10, -10, 5, -5, 0])
    if k % 512:
        return np.exp2(np.random.permutation(np.resize(levels, k // 32))).repeat(32)
    a = np.empty((k // 512, 16))
    for p in range(k // 512):
        a[p, :8] = np.random.permutation(np.resize(levels, 8))
        for g in range(8):
            far = levels[np.abs(levels - a[p, g]) >= 10]
            a[p, g + 8] = far[np.random.randint(len(far))]
    return np.exp2(a.ravel()).repeat(32)


def f64(x):
    return np.asarray(x).astype(np.float64)


def striped(idx):
    return np.tile(idx.reshape(-1, 16).T, (8, 1)).astype(np.uint16)


def unstriped(offs):
    return offs[:16].T.reshape(-1).astype(np.int64)


def pack_weight(w):
    k, n = w.shape
    w = f64(np.asarray(w, np.float32).astype(ml_dtypes.bfloat16)).reshape(k // 32, 32, n)
    amax = np.abs(w).max(1)
    byte = np.clip(np.where(amax > 0, np.frexp(amax)[1] - 1 + 127 - 7, 1), 1, 254)
    scaled = (w * np.exp2(127.0 - byte)[:, None, :]).reshape(k, n).astype(np.float32)
    words = np.ascontiguousarray(scaled.reshape(k // 512, 128, 4, n).transpose(0, 1, 3, 2)).astype(ml_dtypes.float8_e4m3fn).view(np.uint8)
    return words, np.ascontiguousarray(byte.astype(np.uint8).reshape(k // 512, 16, n))


def unpack_weight(words, scales):
    g, p, n, _ = words.shape
    vals = np.ascontiguousarray(words).view(ml_dtypes.float8_e4m3fn).astype(np.float64) * np.repeat(np.exp2(scales.astype(np.float64) - 127.0), 8, axis=1)[..., None]
    return vals.transpose(0, 1, 3, 2).reshape(g * 512, n)


E2M1 = np.array([0.0, 0.5, 1.0, 1.5, 2.0, 3.0, 4.0, 6.0, -0.0, -0.5, -1.0, -1.5, -2.0, -3.0, -4.0, -6.0])


def pack_fp4(w):
    k, n = w.shape
    w = f64(np.asarray(w, np.float32).astype(ml_dtypes.bfloat16)).reshape(k // 32, 32, n)
    amax = np.abs(w).max(1)
    mant, ex = np.frexp(amax / 6.0)
    byte = np.clip(np.where(amax > 0, np.where(mant > 0.5, ex, ex - 1) + 127, 1), 1, 254)
    scaled = (w * np.exp2(127.0 - byte)[:, None, :]).reshape(k, n).astype(np.float32)
    c = np.ascontiguousarray(scaled.reshape(k // 512, 128, 4, n).transpose(0, 1, 3, 2)).astype(ml_dtypes.float4_e2m1fn).view(np.uint8) & 0xF
    words = (c[..., 0::2] | (c[..., 1::2] << 4)).reshape(k // 512, 128, 2 * n)
    return np.ascontiguousarray(words), np.ascontiguousarray(byte.astype(np.uint8).reshape(k // 512, 16, n))


def unpack_fp4(words, scales):
    g, _, n = scales.shape
    words = np.ascontiguousarray(words).reshape(g, 128, n, 2)
    nib = np.empty((g, 128, n, 4), np.uint8)
    nib[..., 0::2] = words & 0xF
    nib[..., 1::2] = words >> 4
    vals = E2M1[nib] * np.repeat(np.exp2(scales.astype(np.float64) - 127.0), 8, axis=1)[..., None]
    return vals.transpose(0, 1, 3, 2).reshape(g * 512, n)


def relu(v):
    return np.maximum(v, 0.0)


K, T, S, N, H = 512, 1024, 512, 128, 512


def setup_inputs():
    n = np.random.standard_normal
    s = mx_kscale(K)[:, None]
    u = mx_kscale(H)
    packed_xT = pack_weight(n((K, T)) * s)
    packed_w1 = pack_fp4(n((K, H)) / np.sqrt(K) / s)
    packed_w2 = pack_fp4(n((H, N)) / np.sqrt(H) / u[:, None])
    return {
        "x_words": packed_xT[0],
        "x_scales": packed_xT[1],
        "w1_words": packed_w1[0],
        "w1_scales": packed_w1[1],
        "rdy": (np.random.uniform(0.0, 1.0, (H, S))).astype(np.float32),
        "unit": (np.random.uniform(0.6, 1.4, (H, 1)) * u[:, None]).astype(np.float32),
        "w2_words": packed_w2[0],
        "w2_scales": packed_w2[1],
        "offs": striped(np.random.permutation(T)[:S]),
        "pr1": striped(np.random.permutation(S)),
        "pr2": striped(np.random.permutation(S)),
        "suc": striped(np.random.permutation(S)),
    }


def reference(x_words, x_scales, w1_words, w1_scales, rdy, unit, w2_words, w2_scales, offs, pr1, pr2, suc):
    xq = unpack_weight(x_words, x_scales)[:, unstriped(offs)]
    y = unpack_fp4(w1_words, w1_scales).T @ xq
    dur = np.log(np.exp(y) + 1.0)
    fin0 = dur + f64(rdy)
    fa = fin0[:, unstriped(pr1)]
    fb = fin0[:, unstriped(pr2)]
    fin1 = dur + np.maximum(fa, fb)
    fc = fin1[:, unstriped(pr1)]
    fd = fin1[:, unstriped(pr2)]
    fin2 = dur + np.maximum(fc, fd)
    fs = fin2[:, unstriped(suc)]
    slk = fs - dur - (0.8 * fin2)
    crit = np.exp(-1.0 * relu(slk))
    hid = f64(unit) * (crit * dur)
    return unpack_fp4(w2_words, w2_scales).T @ mxq(hid, 0, "e4m3")

@@ -1,0 +1,246 @@
+from contextlib import ExitStack
+
+import concourse.mybir as mybir
+
+K, T, S, N, H = 512, 1024, 512, 128, 512
+FLOPS = 2 * K * H * S + 2 * H * N * S
+
+F32 = mybir.dt.float32
+BF16 = mybir.dt.bfloat16
+I32 = mybir.dt.int32
+U32 = mybir.dt.uint32
+U16 = mybir.dt.uint16
+U8 = mybir.dt.uint8
+FP8X4 = mybir.dt.float8_e4m3fn_x4
+FP4X4 = mybir.dt.float4_e2m1fn_x4
+ALU = mybir.AluOpType
+ACT = mybir.ActivationFunctionType
+
+P = 128
+PACK = 4
+HALF = S // 2
+SPARE = 8
+LINEAR_FROM = 40.0
+RING = 3
+SOFT = 2
+TEXT = "L0 D0 F0 L1 D1 F1 L2 D2 F2 L3 D3 F3 P00 P01 m00 a02 f10 b02 m01 P10 x02 f11 P03 m10 f20 P11 m03 C0 f13 k0 m11 P12 f21 C1 m12 P13 k1 f22 m13 C2 f23 U0 U1 U2 U3 g30 g31 X00 X01 K20 C3 K21 H00 s30 s31 X10 X11 H01 H10 I0 H11 Q0 I1 Q1"
+
+
+def tile_picked_ycritp_crit_p_kernel(
+    tc, x_words, x_scales, w1_words, w1_scales, rdy, unit, w2_words, w2_scales, offs, pr1, pr2, suc, out
+):
+    nc = tc.nc
+    with ExitStack() as ctx:
+        keep = ctx.enter_context(tc.tile_pool(name="keep", bufs=1))
+        psum = ctx.enter_context(tc.psum_pool(name="psum", bufs=1))
+
+        def load_list(name, src):
+            tile = keep.tile([P, S // 16], U16, name=name)
+            nc.sync.dma_start(tile[:], src)
+            return tile
+
+        xs = keep.tile([P, T], U8, name="xs", align_bytes=64)
+        w1s_raw = keep.tile([P, H], U8, name="w1s_raw", tag="small", align_bytes=64)
+        w2s = keep.tile([P, N], U8, name="w2s", align_bytes=64)
+
+        def fill_scale_rows(queue, plane, src, quadrants):
+            for q in quadrants:
+                rows = src[0][4 * q : 4 * q + 4, :].bitcast(I32)
+                queue.dma_start(plane[32 * q : 32 * q + 32, :].bitcast(I32), rows.partition_broadcast(8))
+
+        offs_sb = load_list("offs_sb", offs)
+        w1_raw = keep.tile([P, 2 * H], U8, name="w1_raw", tag="large", align_bytes=64)
+        xw = keep.tile([P, T], U32, name="xw", align_bytes=64)
+        fill_scale_rows(nc.sync, xs, x_scales, (0, 1))
+        nc.sync.dma_start(w1_raw[:].bitcast(I32), w1_words[0].bitcast(I32))
+        nc.sync.dma_start(xw[:].bitcast(I32), x_words[0].rearrange("p n t -> p (n t)").bitcast(I32))
+        fill_scale_rows(nc.sync, xs, x_scales, (2, 3))
+        fill_scale_rows(nc.sync, w1s_raw, w1_scales, range(4))
+        pr1_sb = load_list("pr1_sb", pr1)
+        pr2_sb = load_list("pr2_sb", pr2)
+        suc_sb = load_list("suc_sb", suc)
+
+        w1w = keep.tile([P, 2 * H], U8, name="w1w", align_bytes=64)
+        w1s = keep.tile([P, H], U8, name="w1s", align_bytes=64)
+        nc.vector.tensor_copy(
+            w1w[:].rearrange("p (t m b) -> p t m b", t=PACK, b=2),
+            w1_raw[:].rearrange("p (m t b) -> p t m b", t=PACK, b=2),
+        )
+        nc.vector.tensor_copy(
+            w1s[:].rearrange("p (t m) -> p t m", t=PACK), w1s_raw[:].rearrange("p (m t) -> p t m", t=PACK)
+        )
+        plain = keep.tile([P, PACK * S + PACK], F32, name="plain", tag="large", align_bytes=64)
+        rdy_sb = plain[:, : PACK * S].rearrange("p (t j) -> p t j", t=PACK)
+        unit_sb = plain[:, PACK * S :]
+        nc.sync.dma_start(rdy_sb, rdy.rearrange("(p t) j -> p t j", t=PACK))
+        nc.sync.dma_start(unit_sb, unit.rearrange("(p t) o -> p (t o)", t=PACK))
+        w2w = keep.tile([P, 2 * N], U8, name="w2w", align_bytes=64)
+        nc.sync.dma_start(w2w[:].bitcast(I32), w2_words[0].bitcast(I32))
+        fill_scale_rows(nc.sync, w2s, w2_scales, range(4))
+
+        def window(name):
+            tile = keep.tile([P, S + SPARE], F32, name=name)
+            nc.gpsimd.memset(tile[:, S:], 0.0)
+            return tile
+
+        fin = [[window("fin%d_%d" % (r, t)) for t in range(PACK)] for r in range(3)]
+
+        def cols(h):
+            return slice(h * HALF, (h + 1) * HALF)
+
+        def part(lst, h):
+            return lst[:, h * HALF // 16 : (h + 1) * HALF // 16]
+
+        y = {}
+        ey = [keep.tile([P, 2, S], F32, name="ey%d" % u) for u in range(2)]
+        for h in range(2):
+            gw = keep.tile([P, HALF], U32, name="gw%d" % h, align_bytes=64)
+            gs = keep.tile([P, HALF], U8, name="gs%d" % h, tag=("gs0", "small")[h], align_bytes=64)
+            nc.vector.tensor_copy(gw[:], xw[:].indirect(part(offs_sb, h)))
+            nc.vector.tensor_copy(gs[:], xs[:].indirect(part(offs_sb, h)))
+            for u in ((0, 1), (1, 0))[h]:
+                bank = psum.tile([P, 2, HALF], F32, name="bank%d" % (2 * h + u))
+                y[u, h] = bank
+                for e in range(2):
+                    t = 2 * u + e
+                    nc.tensor.matmul_mx(
+                        out=bank[:, e, :],
+                        lhsT=w1w[:, 2 * P * t : 2 * P * (t + 1)].bitcast(FP4X4),
+                        lhsT_scale=w1s[:, P * t : P * (t + 1)],
+                        rhs=gw[:].bitcast(FP8X4),
+                        rhs_scale=gs[:],
+                        start=True,
+                        stop=True,
+                    )
+                nc.scalar.activation(ey[u][:, :, cols(h)], bank[:], ACT.Exp)
+
+        dur = [keep.tile([P, S], F32, name="dur%d" % t) for t in range(PACK)]
+        soft = [keep.tile([P, S], F32, name="soft%d" % i) for i in range(SOFT)]
+        ring = [keep.tile([P, 2, S], F32, name="ring%d" % i) for i in range(RING)]
+        taken = []
+        pair = {}
+        later = {}
+        own = {}
+        weighted = {}
+        crit = {}
+        slack = [keep.tile([P, 2, S], F32, name="slack%d" % u) for u in range(2)]
+        fs = keep.tile([P, PACK, S], F32, name="fs")
+        pairs = [keep.tile([P, 2, 2 * HALF], BF16, name="pairs%d" % h) for h in range(2)]
+        hid = {}
+
+        def take():
+            taken.append(1)
+            return ring[(len(taken) - 1) % RING]
+
+        for word in TEXT.split():
+            k = word[0]
+            a = [int(c) for c in word[1:]]
+            if k == "L":
+                t = a[0]
+                nc.scalar.activation(soft[t % SOFT][:], ey[t // 2][:, t % 2, :], ACT.Ln, bias=1.0)
+            elif k == "D":
+                t = a[0]
+                for h in range(2):
+                    nc.vector.scalar_tensor_tensor(
+                        dur[t][:, cols(h)], soft[t % SOFT][:, cols(h)], LINEAR_FROM, y[t // 2, h][:, t % 2, :], ALU.min, ALU.max
+                    )
+            elif k == "F":
+                t = a[0]
+                nc.vector.tensor_tensor(fin[0][t][:, :S], dur[t][:], rdy_sb[:, t, :], ALU.add)
+            elif k == "P":
+                r, t = a
+                pair[r, t] = take()
+                nc.scalar.activation(pair[r, t][:, 0, :], fin[r][t][:].indirect(pr1_sb[:]), ACT.Copy)
+                nc.scalar.activation(pair[r, t][:, 1, :], fin[r][t][:].indirect(pr2_sb[:]), ACT.Copy)
+            elif k == "m":
+                r, t = a
+                later[r, t] = keep.tile([P, S], F32, name="later%d_%d" % (r, t))
+                nc.vector.tensor_tensor(later[r, t][:], pair[r, t][:, 0, :], pair[r, t][:, 1, :], ALU.max)
+            elif k == "f":
+                r, t = a
+                nc.vector.tensor_tensor(fin[r][t][:, :S], later[r - 1, t][:], dur[t][:], ALU.add)
+            elif k == "a":
+                r, t = a
+                pair[r, t] = keep.tile([P, 2, S], F32, name="both%d_%d" % (r, t))
+                nc.vector.tensor_tensor(pair[r, t][:, 0, :], fin[r][t][:].indirect(pr1_sb[:]), dur[t][:], ALU.add)
+            elif k == "b":
+                r, t = a
+                nc.vector.tensor_tensor(pair[r, t][:, 1, :], fin[r][t][:].indirect(pr2_sb[:]), dur[t][:], ALU.add)
+            elif k == "x":
+                r, t = a
+                nc.vector.tensor_tensor(fin[r + 1][t][:, :S], pair[r, t][:, 0, :], pair[r, t][:, 1, :], ALU.max)
+            elif k == "U":
+                t = a[0]
+                if t % 2 == 0:
+                    weighted[t // 2] = take()
+                nc.scalar.activation(weighted[t // 2][:, t % 2, :], dur[t][:], ACT.Copy, scale=unit_sb[:, t : t + 1])
+            elif k == "u":
+                t = a[0]
+                if t % 2 == 0:
+                    weighted[t // 2] = keep.tile([P, 2, S], F32, name="weighted%d" % t)
+                nc.vector.tensor_scalar(weighted[t // 2][:, t % 2, :], dur[t][:], unit_sb[:, t : t + 1], None, ALU.mult)
+            elif k == "C":
+                t = a[0]
+                own[t] = keep.tile([P, S], F32, name="own%d" % t)
+                nc.vector.scalar_tensor_tensor(own[t][:], fin[2][t][:, :S], -0.8, dur[t][:], ALU.mult, ALU.subtract)
+            elif k == "K":
+                t, h = a
+                nc.vector.tensor_tensor(
+                    slack[t // 2][:, t % 2, cols(h)], fin[2][t][:].indirect(part(suc_sb, h)), own[t][:, cols(h)], ALU.add
+                )
+            elif k == "k":
+                t = a[0]
+                nc.vector.tensor_tensor(slack[t // 2][:, t % 2, :], fin[2][t][:].indirect(suc_sb[:]), own[t][:], ALU.add)
+            elif k == "g":
+                t, h = a
+                nc.scalar.activation(fs[:, t, cols(h)], fin[2][t][:].indirect(part(suc_sb, h)), ACT.Copy)
+            elif k == "s":
+                t, h = a
+                nc.vector.tensor_tensor(slack[t // 2][:, t % 2, cols(h)], fs[:, t, cols(h)], own[t][:, cols(h)], ALU.add)
+            elif k == "X":
+                u, h = a
+                crit[u, h] = keep.tile([P, HALF, 2], F32, name="crit%d_%d" % (u, h))
+                nc.scalar.activation(
+                    crit[u, h][:], slack[u][:, :, cols(h)].rearrange("p e c -> p c e"), ACT.Exp, scale=-1.0
+                )
+            elif k == "H":
+                u, h = a
+                nc.vector.scalar_tensor_tensor(
+                    pairs[h][:, u, :].rearrange("p (c e) -> p c e", e=2),
+                    crit[u, h][:],
+                    1.0,
+                    weighted[u][:, :, cols(h)].rearrange("p e c -> p c e"),
+                    ALU.min,
+                    ALU.mult,
+                )
+            elif k == "I" or k == "J":
+                h = a[0]
+                hid[h] = keep.tile([P, HALF * PACK], BF16, name="hid%d" % h, align_bytes=64)
+                if k == "I":
+                    nc.vector.tensor_copy(
+                        hid[h][:].bitcast(I32).rearrange("p (c u) -> p c u", u=2),
+                        pairs[h][:].bitcast(I32).rearrange("p u c -> p c u"),
+                    )
+                else:
+                    nc.scalar.copy(
+                        hid[h][:].bitcast(U32).rearrange("p (c u) -> p c u", u=2),
+                        pairs[h][:].bitcast(U32).rearrange("p u c -> p c u"),
+                    )
+            elif k == "Q":
+                h = a[0]
+                hw = keep.tile([P, HALF], U32, name="hw%d" % h, align_bytes=64)
+                hs = keep.tile([P, HALF], U8, name="hs%d" % h, align_bytes=64)
+                nc.vector.quantize_mx(out=hw[:].bitcast(FP8X4), scales=hs[:], in_=hid[h][:])
+                bank = psum.tile([P, HALF], F32, name="out%d" % h)
+                nc.tensor.matmul_mx(
+                    out=bank[:],
+                    lhsT=w2w[:].bitcast(FP4X4),
+                    lhsT_scale=w2s[:],
+                    rhs=hw[:].bitcast(FP8X4),
+                    rhs_scale=hs[:],
+                    start=True,
+                    stop=True,
+                )
+                result = keep.tile([P, HALF], F32, name="result%d" % h)
+                nc.scalar.copy(result[:], bank[:])
+                nc.sync.dma_start(out[:, cols(h)], result[:])

@@ -22,8 +22,8 @@ HALF = S // 2
 SPARE = 8
 LINEAR_FROM = 40.0
 RING = 3
-SOFT = 2
-TEXT = "L0 D0 F0 L1 D1 F1 L2 D2 F2 L3 D3 F3 P00 P01 m00 a02 f10 b02 m01 P10 x02 f11 P03 m10 f20 P11 m03 C0 f13 k0 m11 P12 f21 C1 m12 P13 k1 f22 m13 C2 f23 U0 U1 U2 U3 g30 g31 X00 X01 K20 C3 K21 H00 s30 s31 X10 X11 H01 H10 I0 H11 Q0 I1 Q1"
+SOFT = 4
+TEXT = "L0 D0 u0 F0 L1 D1 u1 F1 L2 D2 u2 F2 L3 D3 u3 F3 P00 P01 m00 f10 a02 b02 P10 m01 f11 P03 P11 x02 m10 f20 C0 k0 P12 m03 f13 m11 f21 C1 k1 P13 m12 f22 C2 G2 m13 f23 C3 X00 X01 H00 H01 g30 g31 S2 s30 X10 H10 I0 Q0 s31 X11 H11 I1 Q1"
 
 
 def tile_picked_ycritp_crit_p_kernel(
@@ -40,7 +40,7 @@ def tile_picked_ycritp_crit_p_kernel(
             return tile
 
         xs = keep.tile([P, T], U8, name="xs", align_bytes=64)
-        w1s_raw = keep.tile([P, H], U8, name="w1s_raw", tag="small", align_bytes=64)
+        w1s_raw = keep.tile([P, H], U8, name="w1s_raw", align_bytes=64)
         w2s = keep.tile([P, N], U8, name="w2s", align_bytes=64)
 
         def fill_scale_rows(queue, plane, src, quadrants):
@@ -48,13 +48,12 @@ def tile_picked_ycritp_crit_p_kernel(
                 rows = src[0][4 * q : 4 * q + 4, :].bitcast(I32)
                 queue.dma_start(plane[32 * q : 32 * q + 32, :].bitcast(I32), rows.partition_broadcast(8))
 
-        offs_sb = load_list("offs_sb", offs)
         w1_raw = keep.tile([P, 2 * H], U8, name="w1_raw", tag="large", align_bytes=64)
         xw = keep.tile([P, T], U32, name="xw", align_bytes=64)
-        fill_scale_rows(nc.sync, xs, x_scales, (0, 1))
         nc.sync.dma_start(w1_raw[:].bitcast(I32), w1_words[0].bitcast(I32))
+        offs_sb = load_list("offs_sb", offs)
         nc.sync.dma_start(xw[:].bitcast(I32), x_words[0].rearrange("p n t -> p (n t)").bitcast(I32))
-        fill_scale_rows(nc.sync, xs, x_scales, (2, 3))
+        fill_scale_rows(nc.scalar, xs, x_scales, range(4))
         fill_scale_rows(nc.sync, w1s_raw, w1_scales, range(4))
         pr1_sb = load_list("pr1_sb", pr1)
         pr2_sb = load_list("pr2_sb", pr2)
@@ -66,7 +65,7 @@ def tile_picked_ycritp_crit_p_kernel(
             w1w[:].rearrange("p (t m b) -> p t m b", t=PACK, b=2),
             w1_raw[:].rearrange("p (m t b) -> p t m b", t=PACK, b=2),
         )
-        nc.vector.tensor_copy(
+        nc.gpsimd.tensor_copy(
             w1s[:].rearrange("p (t m) -> p t m", t=PACK), w1s_raw[:].rearrange("p (m t) -> p t m", t=PACK)
         )
         plain = keep.tile([P, PACK * S + PACK], F32, name="plain", tag="large", align_bytes=64)
@@ -91,28 +90,24 @@ def tile_picked_ycritp_crit_p_kernel(
         def part(lst, h):
             return lst[:, h * HALF // 16 : (h + 1) * HALF // 16]
 
-        y = {}
-        ey = [keep.tile([P, 2, S], F32, name="ey%d" % u) for u in range(2)]
+        y = [psum.tile([P, S], F32, name="bank%d" % t) for t in range(PACK)]
+        ey = [keep.tile([P, S], F32, name="ey%d" % t) for t in range(PACK)]
         for h in range(2):
             gw = keep.tile([P, HALF], U32, name="gw%d" % h, align_bytes=64)
-            gs = keep.tile([P, HALF], U8, name="gs%d" % h, tag=("gs0", "small")[h], align_bytes=64)
+            gs = keep.tile([P, HALF], U8, name="gs%d" % h, align_bytes=64)
             nc.vector.tensor_copy(gw[:], xw[:].indirect(part(offs_sb, h)))
             nc.vector.tensor_copy(gs[:], xs[:].indirect(part(offs_sb, h)))
-            for u in ((0, 1), (1, 0))[h]:
-                bank = psum.tile([P, 2, HALF], F32, name="bank%d" % (2 * h + u))
-                y[u, h] = bank
-                for e in range(2):
-                    t = 2 * u + e
-                    nc.tensor.matmul_mx(
-                        out=bank[:, e, :],
-                        lhsT=w1w[:, 2 * P * t : 2 * P * (t + 1)].bitcast(FP4X4),
-                        lhsT_scale=w1s[:, P * t : P * (t + 1)],
-                        rhs=gw[:].bitcast(FP8X4),
-                        rhs_scale=gs[:],
-                        start=True,
-                        stop=True,
-                    )
-                nc.scalar.activation(ey[u][:, :, cols(h)], bank[:], ACT.Exp)
+            for t in range(PACK):
+                nc.tensor.matmul_mx(
+                    out=y[t][:, cols(h)],
+                    lhsT=w1w[:, 2 * P * t : 2 * P * (t + 1)].bitcast(FP4X4),
+                    lhsT_scale=w1s[:, P * t : P * (t + 1)],
+                    rhs=gw[:].bitcast(FP8X4),
+                    rhs_scale=gs[:],
+                    start=True,
+                    stop=True,
+                )
+                nc.scalar.activation(ey[t][:, cols(h)], y[t][:, cols(h)], ACT.Exp)
 
         dur = [keep.tile([P, S], F32, name="dur%d" % t) for t in range(PACK)]
         soft = [keep.tile([P, S], F32, name="soft%d" % i) for i in range(SOFT)]
@@ -137,13 +132,10 @@ def tile_picked_ycritp_crit_p_kernel(
             a = [int(c) for c in word[1:]]
             if k == "L":
                 t = a[0]
-                nc.scalar.activation(soft[t % SOFT][:], ey[t // 2][:, t % 2, :], ACT.Ln, bias=1.0)
+                nc.scalar.activation(soft[t % SOFT][:], ey[t][:], ACT.Ln, bias=1.0)
             elif k == "D":
                 t = a[0]
-                for h in range(2):
-                    nc.vector.scalar_tensor_tensor(
-                        dur[t][:, cols(h)], soft[t % SOFT][:, cols(h)], LINEAR_FROM, y[t // 2, h][:, t % 2, :], ALU.min, ALU.max
-                    )
+                nc.vector.scalar_tensor_tensor(dur[t][:], soft[t % SOFT][:], LINEAR_FROM, y[t][:], ALU.min, ALU.max)
             elif k == "F":
                 t = a[0]
                 nc.vector.tensor_tensor(fin[0][t][:, :S], dur[t][:], rdy_sb[:, t, :], ALU.add)
@@ -178,7 +170,7 @@ def tile_picked_ycritp_crit_p_kernel(
                 t = a[0]
                 if t % 2 == 0:
                     weighted[t // 2] = keep.tile([P, 2, S], F32, name="weighted%d" % t)
-                nc.vector.tensor_scalar(weighted[t // 2][:, t % 2, :], dur[t][:], unit_sb[:, t : t + 1], None, ALU.mult)
+                nc.gpsimd.tensor_scalar(weighted[t // 2][:, t % 2, :], dur[t][:], unit_sb[:, t : t + 1], 0.0, ALU.mult, ALU.add)
             elif k == "C":
                 t = a[0]
                 own[t] = keep.tile([P, S], F32, name="own%d" % t)
@@ -194,6 +186,12 @@ def tile_picked_ycritp_crit_p_kernel(
             elif k == "g":
                 t, h = a
                 nc.scalar.activation(fs[:, t, cols(h)], fin[2][t][:].indirect(part(suc_sb, h)), ACT.Copy)
+            elif k == "G":
+                t = a[0]
+                nc.scalar.activation(fs[:, t, :], fin[2][t][:].indirect(suc_sb[:]), ACT.Copy)
+            elif k == "S":
+                t = a[0]
+                nc.vector.tensor_tensor(slack[t // 2][:, t % 2, :], fs[:, t, :], own[t][:], ALU.add)
             elif k == "s":
                 t, h = a
                 nc.vector.tensor_tensor(slack[t // 2][:, t % 2, cols(h)], fs[:, t, cols(h)], own[t][:, cols(h)], ALU.add)

@@ -17,13 +17,13 @@ ALU = mybir.AluOpType
 ACT = mybir.ActivationFunctionType
 
 P = 128
-PACK = 4
+PLANES = 4
 HALF = S // 2
+PER_COLUMN = 16
 SPARE = 8
 LINEAR_FROM = 40.0
-RING = 3
-SOFT = 4
-TEXT = "L0 D0 u0 F0 L1 D1 u1 F1 L2 D2 u2 F2 L3 D3 u3 F3 P00 P01 m00 f10 a02 b02 P10 m01 f11 P03 P11 x02 m10 f20 C0 k0 P12 m03 f13 m11 f21 C1 k1 P13 m12 f22 C2 G2 m13 f23 C3 X00 X01 H00 H01 g30 g31 S2 s30 X10 H10 I0 Q0 s31 X11 H11 I1 Q1"
+ROUNDS = 2
+VECTOR_PLANE = 2
 
 
 def tile_picked_ycritp_crit_p_kernel(
@@ -32,213 +32,204 @@ def tile_picked_ycritp_crit_p_kernel(
     nc = tc.nc
     with ExitStack() as ctx:
         keep = ctx.enter_context(tc.tile_pool(name="keep", bufs=1))
+        shared = ctx.enter_context(tc.tile_pool(name="shared", bufs=1))
         psum = ctx.enter_context(tc.psum_pool(name="psum", bufs=1))
 
+        def cols(h):
+            return slice(h * HALF, (h + 1) * HALF)
+
+        def entries(list_tile, h):
+            return list_tile[:, h * HALF // PER_COLUMN : (h + 1) * HALF // PER_COLUMN]
+
         def load_list(name, src):
-            tile = keep.tile([P, S // 16], U16, name=name)
+            tile = keep.tile([P, S // PER_COLUMN], U16, name=name)
             nc.sync.dma_start(tile[:], src)
             return tile
 
-        xs = keep.tile([P, T], U8, name="xs", align_bytes=64)
-        w1s_raw = keep.tile([P, H], U8, name="w1s_raw", align_bytes=64)
-        w2s = keep.tile([P, N], U8, name="w2s", align_bytes=64)
-
-        def fill_scale_rows(queue, plane, src, quadrants):
-            for q in quadrants:
+        def load_scales(queue, plane, src):
+            for q in range(4):
                 rows = src[0][4 * q : 4 * q + 4, :].bitcast(I32)
                 queue.dma_start(plane[32 * q : 32 * q + 32, :].bitcast(I32), rows.partition_broadcast(8))
 
-        w1_raw = keep.tile([P, 2 * H], U8, name="w1_raw", tag="large", align_bytes=64)
-        xw = keep.tile([P, T], U32, name="xw", align_bytes=64)
-        nc.sync.dma_start(w1_raw[:].bitcast(I32), w1_words[0].bitcast(I32))
+        w1_raw = shared.tile([P, 3 * H], U8, name="w1_raw", align_bytes=64, offset=0)
+        w1_raw_words, w1_raw_scales = w1_raw[:, : 2 * H], w1_raw[:, 2 * H :]
+        nc.sync.dma_start(w1_raw_words.bitcast(I32), w1_words[0].bitcast(I32))
         offs_sb = load_list("offs_sb", offs)
-        nc.sync.dma_start(xw[:].bitcast(I32), x_words[0].rearrange("p n t -> p (n t)").bitcast(I32))
-        fill_scale_rows(nc.scalar, xs, x_scales, range(4))
-        fill_scale_rows(nc.sync, w1s_raw, w1_scales, range(4))
+        x_word_table = keep.tile([P, T], U32, name="x_word_table", align_bytes=64)
+        nc.sync.dma_start(x_word_table[:].bitcast(I32), x_words[0].rearrange("p n t -> p (n t)").bitcast(I32))
+        x_scale_table = keep.tile([P, T], U8, name="x_scale_table", align_bytes=64)
+        load_scales(nc.scalar, x_scale_table, x_scales)
+        load_scales(nc.sync, w1_raw_scales, w1_scales)
         pr1_sb = load_list("pr1_sb", pr1)
         pr2_sb = load_list("pr2_sb", pr2)
+        rdy_sb = keep.tile([P, PLANES, S], F32, name="rdy_sb")
+        nc.sync.dma_start(rdy_sb[:], rdy.rearrange("(p t) j -> p t j", t=PLANES))
+        unit_sb = keep.tile([P, PLANES], F32, name="unit_sb")
+        nc.sync.dma_start(unit_sb[:], unit.rearrange("(p t) o -> p (t o)", t=PLANES))
         suc_sb = load_list("suc_sb", suc)
+        w2w = keep.tile([P, 2 * N], U8, name="w2w", align_bytes=64)
+        nc.sync.dma_start(w2w[:].bitcast(I32), w2_words[0].bitcast(I32))
+        w2s = keep.tile([P, N], U8, name="w2s", align_bytes=64)
+        load_scales(nc.sync, w2s, w2_scales)
 
         w1w = keep.tile([P, 2 * H], U8, name="w1w", align_bytes=64)
         w1s = keep.tile([P, H], U8, name="w1s", align_bytes=64)
         nc.vector.tensor_copy(
-            w1w[:].rearrange("p (t m b) -> p t m b", t=PACK, b=2),
-            w1_raw[:].rearrange("p (m t b) -> p t m b", t=PACK, b=2),
+            w1w[:].rearrange("p (t m b) -> p t m b", t=PLANES, b=2),
+            w1_raw_words.rearrange("p (m t b) -> p t m b", t=PLANES, b=2),
         )
-        nc.gpsimd.tensor_copy(
-            w1s[:].rearrange("p (t m) -> p t m", t=PACK), w1s_raw[:].rearrange("p (m t) -> p t m", t=PACK)
+        nc.vector.tensor_copy(
+            w1s[:].rearrange("p (t m) -> p t m", t=PLANES), w1_raw_scales.rearrange("p (m t) -> p t m", t=PLANES)
         )
-        plain = keep.tile([P, PACK * S + PACK], F32, name="plain", tag="large", align_bytes=64)
-        rdy_sb = plain[:, : PACK * S].rearrange("p (t j) -> p t j", t=PACK)
-        unit_sb = plain[:, PACK * S :]
-        nc.sync.dma_start(rdy_sb, rdy.rearrange("(p t) j -> p t j", t=PACK))
-        nc.sync.dma_start(unit_sb, unit.rearrange("(p t) o -> p (t o)", t=PACK))
-        w2w = keep.tile([P, 2 * N], U8, name="w2w", align_bytes=64)
-        nc.sync.dma_start(w2w[:].bitcast(I32), w2_words[0].bitcast(I32))
-        fill_scale_rows(nc.sync, w2s, w2_scales, range(4))
 
         def window(name):
             tile = keep.tile([P, S + SPARE], F32, name=name)
             nc.gpsimd.memset(tile[:, S:], 0.0)
             return tile
 
-        fin = [[window("fin%d_%d" % (r, t)) for t in range(PACK)] for r in range(3)]
+        fin = [[window("fin%d_%d" % (r, t)) for t in range(PLANES)] for r in range(ROUNDS + 1)]
 
-        def cols(h):
-            return slice(h * HALF, (h + 1) * HALF)
-
-        def part(lst, h):
-            return lst[:, h * HALF // 16 : (h + 1) * HALF // 16]
-
-        y = [psum.tile([P, S], F32, name="bank%d" % t) for t in range(PACK)]
-        ey = [keep.tile([P, S], F32, name="ey%d" % t) for t in range(PACK)]
+        picked = [
+            (
+                keep.tile([P, HALF], U32, name="picked_words0", align_bytes=64),
+                keep.tile([P, HALF], U8, name="picked_scales0", align_bytes=64),
+            ),
+            (
+                shared.tile([P, HALF], U32, name="picked_words1", align_bytes=64, offset=0),
+                shared.tile([P, HALF], U8, name="picked_scales1", align_bytes=64, offset=2 * H),
+            ),
+        ]
+        y = [psum.tile([P, S], F32, name="y%d" % t) for t in range(PLANES)]
+        exp_y = [keep.tile([P, S], F32, name="exp_y%d" % t) for t in range(PLANES)]
         for h in range(2):
-            gw = keep.tile([P, HALF], U32, name="gw%d" % h, align_bytes=64)
-            gs = keep.tile([P, HALF], U8, name="gs%d" % h, align_bytes=64)
-            nc.vector.tensor_copy(gw[:], xw[:].indirect(part(offs_sb, h)))
-            nc.vector.tensor_copy(gs[:], xs[:].indirect(part(offs_sb, h)))
-            for t in range(PACK):
+            words, scales = picked[h]
+            nc.vector.tensor_copy(words[:], x_word_table[:].indirect(entries(offs_sb, h)))
+            nc.vector.tensor_copy(scales[:], x_scale_table[:].indirect(entries(offs_sb, h)))
+            for t in range(PLANES):
                 nc.tensor.matmul_mx(
                     out=y[t][:, cols(h)],
                     lhsT=w1w[:, 2 * P * t : 2 * P * (t + 1)].bitcast(FP4X4),
                     lhsT_scale=w1s[:, P * t : P * (t + 1)],
-                    rhs=gw[:].bitcast(FP8X4),
-                    rhs_scale=gs[:],
+                    rhs=words[:].bitcast(FP8X4),
+                    rhs_scale=scales[:],
                     start=True,
                     stop=True,
                 )
-                nc.scalar.activation(ey[t][:, cols(h)], y[t][:, cols(h)], ACT.Exp)
+                nc.scalar.activation(exp_y[t][:, cols(h)], y[t][:, cols(h)], ACT.Exp)
 
-        dur = [keep.tile([P, S], F32, name="dur%d" % t) for t in range(PACK)]
-        soft = [keep.tile([P, S], F32, name="soft%d" % i) for i in range(SOFT)]
-        ring = [keep.tile([P, 2, S], F32, name="ring%d" % i) for i in range(RING)]
-        taken = []
-        pair = {}
+        dur = [keep.tile([P, S], F32, name="dur%d" % t) for t in range(PLANES)]
+        for t in range(PLANES):
+            soft = keep.tile([P, S], F32, name="soft%d" % t)
+            nc.scalar.activation(soft[:], exp_y[t][:], ACT.Ln, bias=1.0)
+            nc.vector.scalar_tensor_tensor(dur[t][:], soft[:], LINEAR_FROM, y[t][:], ALU.min, ALU.max)
+            nc.vector.tensor_tensor(fin[0][t][:, :S], dur[t][:], rdy_sb[:, t, :], ALU.add)
+
+        fetched = {}
         later = {}
-        own = {}
-        weighted = {}
-        crit = {}
-        slack = [keep.tile([P, 2, S], F32, name="slack%d" % u) for u in range(2)]
-        fs = keep.tile([P, PACK, S], F32, name="fs")
-        pairs = [keep.tile([P, 2, 2 * HALF], BF16, name="pairs%d" % h) for h in range(2)]
-        hid = {}
+        pair_tiles = lambda name: [keep.tile([P, 2, S], F32, name="%s%d" % (name, u)) for u in range(2)]
+        own, slack, weighted = pair_tiles("own"), pair_tiles("slack"), pair_tiles("weighted")
+        successor = keep.tile([P, 2, S], F32, name="successor")
+        woven = [keep.tile([P, 2, 2 * HALF], BF16, name="woven%d" % h) for h in range(2)]
+        predecessors = (pr1_sb, pr2_sb)
 
-        def take():
-            taken.append(1)
-            return ring[(len(taken) - 1) % RING]
+        def scalar_fetch(r, t):
+            fetched[r, t] = keep.tile([P, 2, S], F32, name="fetched%d_%d" % (r, t))
+            for e in range(2):
+                nc.scalar.activation(fetched[r, t][:, e, :], fin[r][t][:].indirect(predecessors[e][:]), ACT.Copy)
 
-        for word in TEXT.split():
-            k = word[0]
-            a = [int(c) for c in word[1:]]
-            if k == "L":
-                t = a[0]
-                nc.scalar.activation(soft[t % SOFT][:], ey[t][:], ACT.Ln, bias=1.0)
-            elif k == "D":
-                t = a[0]
-                nc.vector.scalar_tensor_tensor(dur[t][:], soft[t % SOFT][:], LINEAR_FROM, y[t][:], ALU.min, ALU.max)
-            elif k == "F":
-                t = a[0]
-                nc.vector.tensor_tensor(fin[0][t][:, :S], dur[t][:], rdy_sb[:, t, :], ALU.add)
-            elif k == "P":
-                r, t = a
-                pair[r, t] = take()
-                nc.scalar.activation(pair[r, t][:, 0, :], fin[r][t][:].indirect(pr1_sb[:]), ACT.Copy)
-                nc.scalar.activation(pair[r, t][:, 1, :], fin[r][t][:].indirect(pr2_sb[:]), ACT.Copy)
-            elif k == "m":
-                r, t = a
-                later[r, t] = keep.tile([P, S], F32, name="later%d_%d" % (r, t))
-                nc.vector.tensor_tensor(later[r, t][:], pair[r, t][:, 0, :], pair[r, t][:, 1, :], ALU.max)
-            elif k == "f":
-                r, t = a
-                nc.vector.tensor_tensor(fin[r][t][:, :S], later[r - 1, t][:], dur[t][:], ALU.add)
-            elif k == "a":
-                r, t = a
-                pair[r, t] = keep.tile([P, 2, S], F32, name="both%d_%d" % (r, t))
-                nc.vector.tensor_tensor(pair[r, t][:, 0, :], fin[r][t][:].indirect(pr1_sb[:]), dur[t][:], ALU.add)
-            elif k == "b":
-                r, t = a
-                nc.vector.tensor_tensor(pair[r, t][:, 1, :], fin[r][t][:].indirect(pr2_sb[:]), dur[t][:], ALU.add)
-            elif k == "x":
-                r, t = a
-                nc.vector.tensor_tensor(fin[r + 1][t][:, :S], pair[r, t][:, 0, :], pair[r, t][:, 1, :], ALU.max)
-            elif k == "U":
-                t = a[0]
-                if t % 2 == 0:
-                    weighted[t // 2] = take()
-                nc.scalar.activation(weighted[t // 2][:, t % 2, :], dur[t][:], ACT.Copy, scale=unit_sb[:, t : t + 1])
-            elif k == "u":
-                t = a[0]
-                if t % 2 == 0:
-                    weighted[t // 2] = keep.tile([P, 2, S], F32, name="weighted%d" % t)
-                nc.gpsimd.tensor_scalar(weighted[t // 2][:, t % 2, :], dur[t][:], unit_sb[:, t : t + 1], 0.0, ALU.mult, ALU.add)
-            elif k == "C":
-                t = a[0]
-                own[t] = keep.tile([P, S], F32, name="own%d" % t)
-                nc.vector.scalar_tensor_tensor(own[t][:], fin[2][t][:, :S], -0.8, dur[t][:], ALU.mult, ALU.subtract)
-            elif k == "K":
-                t, h = a
-                nc.vector.tensor_tensor(
-                    slack[t // 2][:, t % 2, cols(h)], fin[2][t][:].indirect(part(suc_sb, h)), own[t][:, cols(h)], ALU.add
-                )
-            elif k == "k":
-                t = a[0]
-                nc.vector.tensor_tensor(slack[t // 2][:, t % 2, :], fin[2][t][:].indirect(suc_sb[:]), own[t][:], ALU.add)
-            elif k == "g":
-                t, h = a
-                nc.scalar.activation(fs[:, t, cols(h)], fin[2][t][:].indirect(part(suc_sb, h)), ACT.Copy)
-            elif k == "G":
-                t = a[0]
-                nc.scalar.activation(fs[:, t, :], fin[2][t][:].indirect(suc_sb[:]), ACT.Copy)
-            elif k == "S":
-                t = a[0]
-                nc.vector.tensor_tensor(slack[t // 2][:, t % 2, :], fs[:, t, :], own[t][:], ALU.add)
-            elif k == "s":
-                t, h = a
-                nc.vector.tensor_tensor(slack[t // 2][:, t % 2, cols(h)], fs[:, t, cols(h)], own[t][:, cols(h)], ALU.add)
-            elif k == "X":
-                u, h = a
-                crit[u, h] = keep.tile([P, HALF, 2], F32, name="crit%d_%d" % (u, h))
-                nc.scalar.activation(
-                    crit[u, h][:], slack[u][:, :, cols(h)].rearrange("p e c -> p c e"), ACT.Exp, scale=-1.0
-                )
-            elif k == "H":
-                u, h = a
+        def take_later(r, t):
+            later[r, t] = keep.tile([P, S], F32, name="later%d_%d" % (r, t))
+            nc.vector.tensor_tensor(later[r, t][:], fetched[r, t][:, 0, :], fetched[r, t][:, 1, :], ALU.max)
+
+        def add_duration(r, t):
+            nc.vector.tensor_tensor(fin[r + 1][t][:, :S], later[r, t][:], dur[t][:], ALU.add)
+
+        finishes = keep.tile([P, 2, S], F32, name="finishes")
+
+        def vector_fetch(e):
+            t = VECTOR_PLANE
+            nc.vector.tensor_tensor(finishes[:, e, :], fin[0][t][:].indirect(predecessors[e][:]), dur[t][:], ALU.add)
+
+        def vector_later():
+            nc.vector.tensor_tensor(fin[1][VECTOR_PLANE][:, :S], finishes[:, 0, :], finishes[:, 1, :], ALU.max)
+
+        def weigh(t):
+            nc.vector.tensor_scalar(weighted[t // 2][:, t % 2, :], dur[t][:], unit_sb[:, t : t + 1], None, ALU.mult)
+
+        def own_part(t):
+            if t < 2:
+                nc.vector.scalar_tensor_tensor(own[0][:, t, :], fin[ROUNDS][t][:, :S], -0.8, dur[t][:], ALU.mult, ALU.subtract)
+            else:
                 nc.vector.scalar_tensor_tensor(
-                    pairs[h][:, u, :].rearrange("p (c e) -> p c e", e=2),
-                    crit[u, h][:],
-                    1.0,
-                    weighted[u][:, :, cols(h)].rearrange("p e c -> p c e"),
-                    ALU.min,
-                    ALU.mult,
+                    own[1][:, t - 2, :], later[ROUNDS - 1, t][:], 0.8 / 1.8, dur[t][:], ALU.mult, ALU.add
                 )
-            elif k == "I" or k == "J":
-                h = a[0]
-                hid[h] = keep.tile([P, HALF * PACK], BF16, name="hid%d" % h, align_bytes=64)
-                if k == "I":
-                    nc.vector.tensor_copy(
-                        hid[h][:].bitcast(I32).rearrange("p (c u) -> p c u", u=2),
-                        pairs[h][:].bitcast(I32).rearrange("p u c -> p c u"),
-                    )
-                else:
-                    nc.scalar.copy(
-                        hid[h][:].bitcast(U32).rearrange("p (c u) -> p c u", u=2),
-                        pairs[h][:].bitcast(U32).rearrange("p u c -> p c u"),
-                    )
-            elif k == "Q":
-                h = a[0]
-                hw = keep.tile([P, HALF], U32, name="hw%d" % h, align_bytes=64)
-                hs = keep.tile([P, HALF], U8, name="hs%d" % h, align_bytes=64)
-                nc.vector.quantize_mx(out=hw[:].bitcast(FP8X4), scales=hs[:], in_=hid[h][:])
-                bank = psum.tile([P, HALF], F32, name="out%d" % h)
-                nc.tensor.matmul_mx(
-                    out=bank[:],
-                    lhsT=w2w[:].bitcast(FP4X4),
-                    lhsT_scale=w2s[:],
-                    rhs=hw[:].bitcast(FP8X4),
-                    rhs_scale=hs[:],
-                    start=True,
-                    stop=True,
-                )
-                result = keep.tile([P, HALF], F32, name="result%d" % h)
-                nc.scalar.copy(result[:], bank[:])
-                nc.sync.dma_start(out[:, cols(h)], result[:])
+
+        def vector_slack(t):
+            nc.vector.tensor_tensor(slack[0][:, t, :], fin[ROUNDS][t][:].indirect(suc_sb[:]), own[0][:, t, :], ALU.add)
+
+        def hidden(u, h):
+            crit = keep.tile([P, HALF, 2], F32, name="crit%d_%d" % (u, h))
+            nc.scalar.activation(crit[:], slack[u][:, :, cols(h)].rearrange("p e c -> p c e"), ACT.Exp, scale=-1.0)
+            nc.vector.scalar_tensor_tensor(
+                woven[h][:, u, :].rearrange("p (c e) -> p c e", e=2),
+                crit[:],
+                1.0,
+                weighted[u][:, :, cols(h)].rearrange("p e c -> p c e"),
+                ALU.min,
+                ALU.mult,
+            )
+
+        side_work = [(vector_fetch, 0), (vector_fetch, 1), (weigh, 0), (vector_later,)] + [(weigh, t) for t in range(1, PLANES)]
+        by_scalar = [(r, t) for r in range(ROUNDS) for t in range(PLANES) if (r, t) != (0, VECTOR_PLANE)]
+
+        def side_step():
+            if side_work:
+                call = side_work.pop(0)
+                call[0](*call[1:])
+
+        scalar_fetch(*by_scalar[0])
+        for i, (r, t) in enumerate(by_scalar):
+            take_later(r, t)
+            if r == ROUNDS - 1 and t == PLANES - 1:
+                side_work.append((own_part, t))
+            side_step()
+            add_duration(r, t)
+            side_step()
+            if i + 1 < len(by_scalar):
+                scalar_fetch(*by_scalar[i + 1])
+            if r == ROUNDS - 1 and t < 2:
+                side_work.extend([(own_part, t), (vector_slack, t)])
+            if r == ROUNDS - 1 and t == 2:
+                side_work.append((own_part, t))
+                nc.scalar.activation(successor[:, 0, :], fin[ROUNDS][t][:].indirect(suc_sb[:]), ACT.Copy)
+
+        for h in range(2):
+            hidden(0, h)
+            nc.scalar.activation(successor[:, 1, cols(h)], fin[ROUNDS][3][:].indirect(entries(suc_sb, h)), ACT.Copy)
+            nc.vector.scalar_tensor_tensor(
+                slack[1][:, :, cols(h)], own[1][:, :, cols(h)], -1.8, successor[:, :, cols(h)], ALU.mult, ALU.add
+            )
+        for h in range(2):
+            hidden(1, h)
+        for h in range(2):
+            hid = keep.tile([P, HALF * PLANES], BF16, name="hid%d" % h, align_bytes=64)
+            nc.vector.tensor_copy(
+                hid[:].bitcast(I32).rearrange("p (c u) -> p c u", u=2),
+                woven[h][:].bitcast(I32).rearrange("p u c -> p c u"),
+            )
+            hid_words = keep.tile([P, HALF], U32, name="hid_words%d" % h, align_bytes=64)
+            hid_scales = keep.tile([P, HALF], U8, name="hid_scales%d" % h, align_bytes=64)
+            nc.vector.quantize_mx(out=hid_words[:].bitcast(FP8X4), scales=hid_scales[:], in_=hid[:])
+            bank = psum.tile([P, HALF], F32, name="out%d" % h)
+            nc.tensor.matmul_mx(
+                out=bank[:],
+                lhsT=w2w[:].bitcast(FP4X4),
+                lhsT_scale=w2s[:],
+                rhs=hid_words[:].bitcast(FP8X4),
+                rhs_scale=hid_scales[:],
+                start=True,
+                stop=True,
+            )
+            result = keep.tile([P, HALF], F32, name="result%d" % h)
+            nc.scalar.copy(result[:], bank[:])
+            nc.sync.dma_start(out[:, cols(h)], result[:])

@@ -17,13 +17,17 @@ ALU = mybir.AluOpType
 ACT = mybir.ActivationFunctionType
 
 P = 128
+QUADRANT = 32
+SCALE_ROWS = 4
 PLANES = 4
+LAST_PLANE = PLANES - 1
 HALF = S // 2
 PER_COLUMN = 16
 SPARE = 8
 LINEAR_FROM = 40.0
 ROUNDS = 2
-VECTOR_PLANE = 2
+OWN_SHARE = 0.8
+OUT_PIECES = ((0, 0, HALF), (1, 0, HALF // 2), (1, HALF // 2, HALF))
 
 
 def tile_picked_ycritp_crit_p_kernel(
@@ -46,10 +50,13 @@ def tile_picked_ycritp_crit_p_kernel(
             nc.sync.dma_start(tile[:], src)
             return tile
 
-        def load_scales(queue, plane, src):
-            for q in range(4):
-                rows = src[0][4 * q : 4 * q + 4, :].bitcast(I32)
-                queue.dma_start(plane[32 * q : 32 * q + 32, :].bitcast(I32), rows.partition_broadcast(8))
+        def load_scales(queue, dst, src):
+            for q in range(P // QUADRANT):
+                rows = src[0][SCALE_ROWS * q : SCALE_ROWS * (q + 1), :].bitcast(I32)
+                queue.dma_start(
+                    dst[QUADRANT * q : QUADRANT * (q + 1), :].bitcast(I32),
+                    rows.partition_broadcast(QUADRANT // SCALE_ROWS),
+                )
 
         w1_raw = shared.tile([P, 3 * H], U8, name="w1_raw", align_bytes=64, offset=0)
         w1_raw_words, w1_raw_scales = w1_raw[:, : 2 * H], w1_raw[:, 2 * H :]
@@ -82,12 +89,12 @@ def tile_picked_ycritp_crit_p_kernel(
             w1s[:].rearrange("p (t m) -> p t m", t=PLANES), w1_raw_scales.rearrange("p (m t) -> p t m", t=PLANES)
         )
 
-        def window(name):
+        def finish_tile(name):
             tile = keep.tile([P, S + SPARE], F32, name=name)
             nc.gpsimd.memset(tile[:, S:], 0.0)
             return tile
 
-        fin = [[window("fin%d_%d" % (r, t)) for t in range(PLANES)] for r in range(ROUNDS + 1)]
+        fin = [[finish_tile("fin%d_%d" % (r, t)) for t in range(PLANES)] for r in range(ROUNDS + 1)]
 
         picked = [
             (
@@ -119,15 +126,24 @@ def tile_picked_ycritp_crit_p_kernel(
 
         dur = [keep.tile([P, S], F32, name="dur%d" % t) for t in range(PLANES)]
         for t in range(PLANES):
-            soft = keep.tile([P, S], F32, name="soft%d" % t)
-            nc.scalar.activation(soft[:], exp_y[t][:], ACT.Ln, bias=1.0)
-            nc.vector.scalar_tensor_tensor(dur[t][:], soft[:], LINEAR_FROM, y[t][:], ALU.min, ALU.max)
-            nc.vector.tensor_tensor(fin[0][t][:, :S], dur[t][:], rdy_sb[:, t, :], ALU.add)
+            log_y = keep.tile([P, S], F32, name="log_y%d" % t)
+            parts = [cols(0), cols(1)] if t == 0 else [slice(0, S)]
+            for part in parts:
+                nc.scalar.activation(log_y[:, part], exp_y[t][:, part], ACT.Ln, bias=1.0)
+                nc.vector.scalar_tensor_tensor(
+                    dur[t][:, part], log_y[:, part], LINEAR_FROM, y[t][:, part], ALU.min, ALU.max
+                )
+            for part in parts:
+                nc.vector.tensor_tensor(fin[0][t][:, part], dur[t][:, part], rdy_sb[:, t, part], ALU.add)
+
+        def pair_tiles(name):
+            return [keep.tile([P, 2, S], F32, name="%s%d" % (name, u)) for u in range(2)]
 
         fetched = {}
         later = {}
-        pair_tiles = lambda name: [keep.tile([P, 2, S], F32, name="%s%d" % (name, u)) for u in range(2)]
-        own, slack, weighted = pair_tiles("own"), pair_tiles("slack"), pair_tiles("weighted")
+        own = pair_tiles("own")
+        slack = pair_tiles("slack")
+        weighted = pair_tiles("weighted")
         successor = keep.tile([P, 2, S], F32, name="successor")
         woven = [keep.tile([P, 2, 2 * HALF], BF16, name="woven%d" % h) for h in range(2)]
         predecessors = (pr1_sb, pr2_sb)
@@ -144,28 +160,30 @@ def tile_picked_ycritp_crit_p_kernel(
         def add_duration(r, t):
             nc.vector.tensor_tensor(fin[r + 1][t][:, :S], later[r, t][:], dur[t][:], ALU.add)
 
-        finishes = keep.tile([P, 2, S], F32, name="finishes")
+        candidates = keep.tile([P, 2, S], F32, name="candidates")
 
         def vector_fetch(e):
-            t = VECTOR_PLANE
-            nc.vector.tensor_tensor(finishes[:, e, :], fin[0][t][:].indirect(predecessors[e][:]), dur[t][:], ALU.add)
+            t = LAST_PLANE
+            nc.vector.tensor_tensor(candidates[:, e, :], fin[0][t][:].indirect(predecessors[e][:]), dur[t][:], ALU.add)
 
         def vector_later():
-            nc.vector.tensor_tensor(fin[1][VECTOR_PLANE][:, :S], finishes[:, 0, :], finishes[:, 1, :], ALU.max)
+            nc.vector.tensor_tensor(fin[1][LAST_PLANE][:, :S], candidates[:, 0, :], candidates[:, 1, :], ALU.max)
 
         def weigh(t):
             nc.vector.tensor_scalar(weighted[t // 2][:, t % 2, :], dur[t][:], unit_sb[:, t : t + 1], None, ALU.mult)
 
-        def own_part(t):
-            if t < 2:
-                nc.vector.scalar_tensor_tensor(own[0][:, t, :], fin[ROUNDS][t][:, :S], -0.8, dur[t][:], ALU.mult, ALU.subtract)
-            else:
-                nc.vector.scalar_tensor_tensor(
-                    own[1][:, t - 2, :], later[ROUNDS - 1, t][:], 0.8 / 1.8, dur[t][:], ALU.mult, ALU.add
-                )
+        def own_of_pair0(t):
+            nc.vector.scalar_tensor_tensor(
+                own[0][:, t, :], fin[ROUNDS][t][:, :S], -OWN_SHARE, dur[t][:], ALU.mult, ALU.subtract
+            )
 
-        def vector_slack(t):
+        def slack_of_pair0(t):
             nc.vector.tensor_tensor(slack[0][:, t, :], fin[ROUNDS][t][:].indirect(suc_sb[:]), own[0][:, t, :], ALU.add)
+
+        def own_of_pair1(t):
+            nc.vector.scalar_tensor_tensor(
+                own[1][:, t % 2, :], later[ROUNDS - 1, t][:], OWN_SHARE / (1 + OWN_SHARE), dur[t][:], ALU.mult, ALU.add
+            )
 
         def hidden(u, h):
             crit = keep.tile([P, HALF, 2], F32, name="crit%d_%d" % (u, h))
@@ -179,8 +197,8 @@ def tile_picked_ycritp_crit_p_kernel(
                 ALU.mult,
             )
 
-        side_work = [(vector_fetch, 0), (vector_fetch, 1), (weigh, 0), (vector_later,)] + [(weigh, t) for t in range(1, PLANES)]
-        by_scalar = [(r, t) for r in range(ROUNDS) for t in range(PLANES) if (r, t) != (0, VECTOR_PLANE)]
+        side_work = [(vector_fetch, e) for e in range(2)] + [(weigh, t) for t in range(PLANES)] + [(vector_later,)]
+        by_scalar = [(r, t) for r in range(ROUNDS) for t in range(PLANES) if (r, t) != (0, LAST_PLANE)]
 
         def side_step():
             if side_work:
@@ -189,38 +207,49 @@ def tile_picked_ycritp_crit_p_kernel(
 
         scalar_fetch(*by_scalar[0])
         for i, (r, t) in enumerate(by_scalar):
+            last_round = r == ROUNDS - 1
             take_later(r, t)
-            if r == ROUNDS - 1 and t == PLANES - 1:
-                side_work.append((own_part, t))
+            if last_round and t == LAST_PLANE:
+                side_work.append((own_of_pair1, t))
             side_step()
             add_duration(r, t)
             side_step()
             if i + 1 < len(by_scalar):
                 scalar_fetch(*by_scalar[i + 1])
-            if r == ROUNDS - 1 and t < 2:
-                side_work.extend([(own_part, t), (vector_slack, t)])
-            if r == ROUNDS - 1 and t == 2:
-                side_work.append((own_part, t))
-                nc.scalar.activation(successor[:, 0, :], fin[ROUNDS][t][:].indirect(suc_sb[:]), ACT.Copy)
+            if last_round and t // 2 == 0:
+                side_work.extend([(own_of_pair0, t), (slack_of_pair0, t)])
+            if last_round and t == LAST_PLANE - 1:
+                side_work.append((own_of_pair1, t))
+                nc.scalar.activation(successor[:, t % 2, :], fin[ROUNDS][t][:].indirect(suc_sb[:]), ACT.Copy)
 
         for h in range(2):
             hidden(0, h)
-            nc.scalar.activation(successor[:, 1, cols(h)], fin[ROUNDS][3][:].indirect(entries(suc_sb, h)), ACT.Copy)
+            nc.scalar.activation(
+                successor[:, LAST_PLANE % 2, cols(h)], fin[ROUNDS][LAST_PLANE][:].indirect(entries(suc_sb, h)), ACT.Copy
+            )
             nc.vector.scalar_tensor_tensor(
-                slack[1][:, :, cols(h)], own[1][:, :, cols(h)], -1.8, successor[:, :, cols(h)], ALU.mult, ALU.add
+                slack[1][:, :, cols(h)],
+                own[1][:, :, cols(h)],
+                -(1 + OWN_SHARE),
+                successor[:, :, cols(h)],
+                ALU.mult,
+                ALU.add,
             )
         for h in range(2):
             hidden(1, h)
-        for h in range(2):
-            hid = keep.tile([P, HALF * PLANES], BF16, name="hid%d" % h, align_bytes=64)
-            nc.vector.tensor_copy(
-                hid[:].bitcast(I32).rearrange("p (c u) -> p c u", u=2),
-                woven[h][:].bitcast(I32).rearrange("p u c -> p c u"),
+
+        for i, (h, lo, hi) in enumerate(OUT_PIECES):
+            width = hi - lo
+            hid = keep.tile([P, width * PLANES], BF16, name="hid%d" % i, align_bytes=64)
+            weave, word = (nc.scalar.copy, U32) if lo == 0 else (nc.vector.tensor_copy, I32)
+            weave(
+                hid[:].bitcast(word).rearrange("p (c u) -> p c u", u=2),
+                woven[h][:].bitcast(word)[:, :, lo:hi].rearrange("p u c -> p c u"),
             )
-            hid_words = keep.tile([P, HALF], U32, name="hid_words%d" % h, align_bytes=64)
-            hid_scales = keep.tile([P, HALF], U8, name="hid_scales%d" % h, align_bytes=64)
+            hid_words = keep.tile([P, width], U32, name="hid_words%d" % i, align_bytes=64)
+            hid_scales = keep.tile([P, width], U8, name="hid_scales%d" % i, align_bytes=64)
             nc.vector.quantize_mx(out=hid_words[:].bitcast(FP8X4), scales=hid_scales[:], in_=hid[:])
-            bank = psum.tile([P, HALF], F32, name="out%d" % h)
+            bank = psum.tile([P, width], F32, name="out%d" % i)
             nc.tensor.matmul_mx(
                 out=bank[:],
                 lhsT=w2w[:].bitcast(FP4X4),
@@ -230,6 +259,6 @@ def tile_picked_ycritp_crit_p_kernel(
                 start=True,
                 stop=True,
             )
-            result = keep.tile([P, HALF], F32, name="result%d" % h)
+            result = keep.tile([P, width], F32, name="result%d" % i)
             nc.scalar.copy(result[:], bank[:])
-            nc.sync.dma_start(out[:, cols(h)], result[:])
+            nc.sync.dma_start(out[:, h * HALF + lo : h * HALF + hi], result[:])

from contextlib import ExitStack

import concourse.mybir as mybir

K, T, S, N, H = 512, 1024, 512, 128, 512
FLOPS = 2 * K * H * S + 2 * H * N * S

F32 = mybir.dt.float32
BF16 = mybir.dt.bfloat16
I32 = mybir.dt.int32
U32 = mybir.dt.uint32
U16 = mybir.dt.uint16
U8 = mybir.dt.uint8
FP8X4 = mybir.dt.float8_e4m3fn_x4
FP4X4 = mybir.dt.float4_e2m1fn_x4
ALU = mybir.AluOpType
ACT = mybir.ActivationFunctionType

P = 128
QUADRANT = 32
SCALE_ROWS = 4
PLANES = 4
LAST_PLANE = PLANES - 1
HALF = S // 2
PER_COLUMN = 16
SPARE = 8
LINEAR_FROM = 40.0
ROUNDS = 2
OWN_SHARE = 0.8
OUT_PIECES = ((0, 0, HALF), (1, 0, HALF // 2), (1, HALF // 2, HALF))


def tile_picked_ycritp_crit_p_kernel(
    tc, x_words, x_scales, w1_words, w1_scales, rdy, unit, w2_words, w2_scales, offs, pr1, pr2, suc, out
):
    nc = tc.nc
    with ExitStack() as ctx:
        keep = ctx.enter_context(tc.tile_pool(name="keep", bufs=1))
        shared = ctx.enter_context(tc.tile_pool(name="shared", bufs=1))
        psum = ctx.enter_context(tc.psum_pool(name="psum", bufs=1))

        def cols(h):
            return slice(h * HALF, (h + 1) * HALF)

        def entries(list_tile, h):
            return list_tile[:, h * HALF // PER_COLUMN : (h + 1) * HALF // PER_COLUMN]

        def load_list(name, src):
            tile = keep.tile([P, S // PER_COLUMN], U16, name=name)
            nc.sync.dma_start(tile[:], src)
            return tile

        def load_scales(queue, dst, src):
            for q in range(P // QUADRANT):
                rows = src[0][SCALE_ROWS * q : SCALE_ROWS * (q + 1), :].bitcast(I32)
                queue.dma_start(
                    dst[QUADRANT * q : QUADRANT * (q + 1), :].bitcast(I32),
                    rows.partition_broadcast(QUADRANT // SCALE_ROWS),
                )

        w1_raw = shared.tile([P, 3 * H], U8, name="w1_raw", align_bytes=64, offset=0)
        w1_raw_words, w1_raw_scales = w1_raw[:, : 2 * H], w1_raw[:, 2 * H :]
        nc.sync.dma_start(w1_raw_words.bitcast(I32), w1_words[0].bitcast(I32))
        offs_sb = load_list("offs_sb", offs)
        x_word_table = keep.tile([P, T], U32, name="x_word_table", align_bytes=64)
        nc.sync.dma_start(x_word_table[:].bitcast(I32), x_words[0].rearrange("p n t -> p (n t)").bitcast(I32))
        x_scale_table = keep.tile([P, T], U8, name="x_scale_table", align_bytes=64)
        load_scales(nc.scalar, x_scale_table, x_scales)
        load_scales(nc.sync, w1_raw_scales, w1_scales)
        pr1_sb = load_list("pr1_sb", pr1)
        pr2_sb = load_list("pr2_sb", pr2)
        rdy_sb = keep.tile([P, PLANES, S], F32, name="rdy_sb")
        nc.sync.dma_start(rdy_sb[:], rdy.rearrange("(p t) j -> p t j", t=PLANES))
        unit_sb = keep.tile([P, PLANES], F32, name="unit_sb")
        nc.sync.dma_start(unit_sb[:], unit.rearrange("(p t) o -> p (t o)", t=PLANES))
        suc_sb = load_list("suc_sb", suc)
        w2w = keep.tile([P, 2 * N], U8, name="w2w", align_bytes=64)
        nc.sync.dma_start(w2w[:].bitcast(I32), w2_words[0].bitcast(I32))
        w2s = keep.tile([P, N], U8, name="w2s", align_bytes=64)
        load_scales(nc.sync, w2s, w2_scales)

        w1w = keep.tile([P, 2 * H], U8, name="w1w", align_bytes=64)
        w1s = keep.tile([P, H], U8, name="w1s", align_bytes=64)
        nc.vector.tensor_copy(
            w1w[:].rearrange("p (t m b) -> p t m b", t=PLANES, b=2),
            w1_raw_words.rearrange("p (m t b) -> p t m b", t=PLANES, b=2),
        )
        nc.vector.tensor_copy(
            w1s[:].rearrange("p (t m) -> p t m", t=PLANES), w1_raw_scales.rearrange("p (m t) -> p t m", t=PLANES)
        )

        def finish_tile(name):
            tile = keep.tile([P, S + SPARE], F32, name=name)
            nc.gpsimd.memset(tile[:, S:], 0.0)
            return tile

        fin = [[finish_tile("fin%d_%d" % (r, t)) for t in range(PLANES)] for r in range(ROUNDS + 1)]

        picked = [
            (
                keep.tile([P, HALF], U32, name="picked_words0", align_bytes=64),
                keep.tile([P, HALF], U8, name="picked_scales0", align_bytes=64),
            ),
            (
                shared.tile([P, HALF], U32, name="picked_words1", align_bytes=64, offset=0),
                shared.tile([P, HALF], U8, name="picked_scales1", align_bytes=64, offset=2 * H),
            ),
        ]
        y = [psum.tile([P, S], F32, name="y%d" % t) for t in range(PLANES)]
        exp_y = [keep.tile([P, S], F32, name="exp_y%d" % t) for t in range(PLANES)]
        for h in range(2):
            words, scales = picked[h]
            nc.vector.tensor_copy(words[:], x_word_table[:].indirect(entries(offs_sb, h)))
            nc.vector.tensor_copy(scales[:], x_scale_table[:].indirect(entries(offs_sb, h)))
            for t in range(PLANES):
                nc.tensor.matmul_mx(
                    out=y[t][:, cols(h)],
                    lhsT=w1w[:, 2 * P * t : 2 * P * (t + 1)].bitcast(FP4X4),
                    lhsT_scale=w1s[:, P * t : P * (t + 1)],
                    rhs=words[:].bitcast(FP8X4),
                    rhs_scale=scales[:],
                    start=True,
                    stop=True,
                )
                nc.scalar.activation(exp_y[t][:, cols(h)], y[t][:, cols(h)], ACT.Exp)

        dur = [keep.tile([P, S], F32, name="dur%d" % t) for t in range(PLANES)]
        for t in range(PLANES):
            log_y = keep.tile([P, S], F32, name="log_y%d" % t)
            parts = [cols(0), cols(1)] if t == 0 else [slice(0, S)]
            for part in parts:
                nc.scalar.activation(log_y[:, part], exp_y[t][:, part], ACT.Ln, bias=1.0)
                nc.vector.scalar_tensor_tensor(
                    dur[t][:, part], log_y[:, part], LINEAR_FROM, y[t][:, part], ALU.min, ALU.max
                )
            for part in parts:
                nc.vector.tensor_tensor(fin[0][t][:, part], dur[t][:, part], rdy_sb[:, t, part], ALU.add)

        def pair_tiles(name):
            return [keep.tile([P, 2, S], F32, name="%s%d" % (name, u)) for u in range(2)]

        fetched = {}
        later = {}
        own = pair_tiles("own")
        slack = pair_tiles("slack")
        weighted = pair_tiles("weighted")
        successor = keep.tile([P, 2, S], F32, name="successor")
        woven = [keep.tile([P, 2, 2 * HALF], BF16, name="woven%d" % h) for h in range(2)]
        predecessors = (pr1_sb, pr2_sb)

        def scalar_fetch(r, t):
            fetched[r, t] = keep.tile([P, 2, S], F32, name="fetched%d_%d" % (r, t))
            for e in range(2):
                nc.scalar.activation(fetched[r, t][:, e, :], fin[r][t][:].indirect(predecessors[e][:]), ACT.Copy)

        def take_later(r, t):
            later[r, t] = keep.tile([P, S], F32, name="later%d_%d" % (r, t))
            nc.vector.tensor_tensor(later[r, t][:], fetched[r, t][:, 0, :], fetched[r, t][:, 1, :], ALU.max)

        def add_duration(r, t):
            nc.vector.tensor_tensor(fin[r + 1][t][:, :S], later[r, t][:], dur[t][:], ALU.add)

        candidates = keep.tile([P, 2, S], F32, name="candidates")

        def vector_fetch(e):
            t = LAST_PLANE
            nc.vector.tensor_tensor(candidates[:, e, :], fin[0][t][:].indirect(predecessors[e][:]), dur[t][:], ALU.add)

        def vector_later():
            nc.vector.tensor_tensor(fin[1][LAST_PLANE][:, :S], candidates[:, 0, :], candidates[:, 1, :], ALU.max)

        def weigh(t):
            nc.vector.tensor_scalar(weighted[t // 2][:, t % 2, :], dur[t][:], unit_sb[:, t : t + 1], None, ALU.mult)

        def own_of_pair0(t):
            nc.vector.scalar_tensor_tensor(
                own[0][:, t, :], fin[ROUNDS][t][:, :S], -OWN_SHARE, dur[t][:], ALU.mult, ALU.subtract
            )

        def slack_of_pair0(t):
            nc.vector.tensor_tensor(slack[0][:, t, :], fin[ROUNDS][t][:].indirect(suc_sb[:]), own[0][:, t, :], ALU.add)

        def own_of_pair1(t):
            nc.vector.scalar_tensor_tensor(
                own[1][:, t % 2, :], later[ROUNDS - 1, t][:], OWN_SHARE / (1 + OWN_SHARE), dur[t][:], ALU.mult, ALU.add
            )

        def hidden(u, h):
            crit = keep.tile([P, HALF, 2], F32, name="crit%d_%d" % (u, h))
            nc.scalar.activation(crit[:], slack[u][:, :, cols(h)].rearrange("p e c -> p c e"), ACT.Exp, scale=-1.0)
            nc.vector.scalar_tensor_tensor(
                woven[h][:, u, :].rearrange("p (c e) -> p c e", e=2),
                crit[:],
                1.0,
                weighted[u][:, :, cols(h)].rearrange("p e c -> p c e"),
                ALU.min,
                ALU.mult,
            )

        side_work = [(vector_fetch, e) for e in range(2)] + [(weigh, t) for t in range(PLANES)] + [(vector_later,)]
        by_scalar = [(r, t) for r in range(ROUNDS) for t in range(PLANES) if (r, t) != (0, LAST_PLANE)]

        def side_step():
            if side_work:
                call = side_work.pop(0)
                call[0](*call[1:])

        scalar_fetch(*by_scalar[0])
        for i, (r, t) in enumerate(by_scalar):
            last_round = r == ROUNDS - 1
            take_later(r, t)
            if last_round and t == LAST_PLANE:
                side_work.append((own_of_pair1, t))
            side_step()
            add_duration(r, t)
            side_step()
            if i + 1 < len(by_scalar):
                scalar_fetch(*by_scalar[i + 1])
            if last_round and t // 2 == 0:
                side_work.extend([(own_of_pair0, t), (slack_of_pair0, t)])
            if last_round and t == LAST_PLANE - 1:
                side_work.append((own_of_pair1, t))
                nc.scalar.activation(successor[:, t % 2, :], fin[ROUNDS][t][:].indirect(suc_sb[:]), ACT.Copy)

        for h in range(2):
            hidden(0, h)
            nc.scalar.activation(
                successor[:, LAST_PLANE % 2, cols(h)], fin[ROUNDS][LAST_PLANE][:].indirect(entries(suc_sb, h)), ACT.Copy
            )
            nc.vector.scalar_tensor_tensor(
                slack[1][:, :, cols(h)],
                own[1][:, :, cols(h)],
                -(1 + OWN_SHARE),
                successor[:, :, cols(h)],
                ALU.mult,
                ALU.add,
            )
        for h in range(2):
            hidden(1, h)

        for i, (h, lo, hi) in enumerate(OUT_PIECES):
            width = hi - lo
            hid = keep.tile([P, width * PLANES], BF16, name="hid%d" % i, align_bytes=64)
            weave, word = (nc.scalar.copy, U32) if lo == 0 else (nc.vector.tensor_copy, I32)
            weave(
                hid[:].bitcast(word).rearrange("p (c u) -> p c u", u=2),
                woven[h][:].bitcast(word)[:, :, lo:hi].rearrange("p u c -> p c u"),
            )
            hid_words = keep.tile([P, width], U32, name="hid_words%d" % i, align_bytes=64)
            hid_scales = keep.tile([P, width], U8, name="hid_scales%d" % i, align_bytes=64)
            nc.vector.quantize_mx(out=hid_words[:].bitcast(FP8X4), scales=hid_scales[:], in_=hid[:])
            bank = psum.tile([P, width], F32, name="out%d" % i)
            nc.tensor.matmul_mx(
                out=bank[:],
                lhsT=w2w[:].bitcast(FP4X4),
                lhsT_scale=w2s[:],
                rhs=hid_words[:].bitcast(FP8X4),
                rhs_scale=hid_scales[:],
                start=True,
                stop=True,
            )
            result = keep.tile([P, width], F32, name="result%d" % i)
            nc.scalar.copy(result[:], bank[:])
            nc.sync.dma_start(out[:, h * HALF + lo : h * HALF + hi], result[:])
